import numpy as np
import ml_dtypes


def mxq(x, axis, fmt="e4m3"):
    dtype, down = {"e4m3": (ml_dtypes.float8_e4m3fn, 7), "e5m2": (ml_dtypes.float8_e5m2, 14)}[fmt]
    v = np.moveaxis(np.asarray(x, np.float32).astype(ml_dtypes.bfloat16).astype(np.float64), axis, -1)
    blocks = v.reshape(v.shape[:-1] + (-1, 32))
    amax = np.abs(blocks).max(-1, keepdims=True)
    byte = np.maximum(np.where(amax > 0, np.frexp(amax)[1] - 1 + 127, 0) - down, 1)
    scale = np.exp2(byte - 127.0)
    codes = (blocks / scale).astype(np.float32).astype(dtype).astype(np.float64)
    return np.moveaxis((codes * scale).reshape(v.shape), -1, axis)


WIDE = False


def mx_kscale(k):
    if not WIDE:
        return np.ones(k)
    levels = np.array([10, -10, 5, -5, 0])
    if k % 512:
        return np.exp2(np.random.permutation(np.resize(levels, k // 32))).repeat(32)
    a = np.empty((k // 512, 16))
    for p in range(k // 512):
        a[p, :8] = np.random.permutation(np.resize(levels, 8))
        for g in range(8):
            far = levels[np.abs(levels - a[p, g]) >= 10]
            a[p, g + 8] = far[np.random.randint(len(far))]
    return np.exp2(a.ravel()).repeat(32)


def f64(x):
    return np.asarray(x).astype(np.float64)


def striped(idx):
    return np.tile(idx.reshape(-1, 16).T, (8, 1)).astype(np.uint16)


def unstriped(offs):
    return offs[:16].T.reshape(-1).astype(np.int64)


E2M1 = np.array([0.0, 0.5, 1.0, 1.5, 2.0, 3.0, 4.0, 6.0, -0.0, -0.5, -1.0, -1.5, -2.0, -3.0, -4.0, -6.0])


def pack_weight(w, fmt):
    k, n = w.shape
    w = f64(np.asarray(w, np.float32).astype(ml_dtypes.bfloat16)).reshape(k // 32, 32, n)
    amax = np.abs(w).max(1)
    if fmt == "e4m3":
        byte = np.frexp(amax)[1] - 1 + 127 - 7
    else:
        mant, ex = np.frexp(amax / 6.0)
        byte = np.where(mant > 0.5, ex, ex - 1) + 127
    byte = np.clip(np.where(amax > 0, byte, 1), 1, 254)
    scaled = (w * np.exp2(127.0 - byte)[:, None, :]).reshape(k, n).astype(np.float32)
    by_word = np.ascontiguousarray(scaled.reshape(k // 512, 128, 4, n).transpose(0, 1, 3, 2))
    if fmt == "e4m3":
        words = by_word.astype(ml_dtypes.float8_e4m3fn).view(np.uint8)
    else:
        c = by_word.astype(ml_dtypes.float4_e2m1fn).view(np.uint8) & 0xF
        words = (c[..., 0::2] | (c[..., 1::2] << 4)).reshape(k // 512, 128, 2 * n)
    return np.ascontiguousarray(words), np.ascontiguousarray(byte.astype(np.uint8).reshape(k // 512, 16, n))


def unpack_weight(words, scales, fmt):
    g, _, n = scales.shape
    words = np.ascontiguousarray(words).reshape(g, 128, n, -1)
    if fmt == "e4m3":
        vals = words.view(ml_dtypes.float8_e4m3fn).astype(np.float64)
    else:
        nib = np.empty((g, 128, n, 4), np.uint8)
        nib[..., 0::2] = words & 0xF
        nib[..., 1::2] = words >> 4
        vals = E2M1[nib]
    vals = vals * np.repeat(np.exp2(scales.astype(np.float64) - 127.0), 8, axis=1)[..., None]
    return vals.transpose(0, 1, 3, 2).reshape(g * 512, n)


def gelu(v):
    return 0.5 * v * (1.0 + np.tanh(np.sqrt(2.0 / np.pi) * (v + 0.044715 * v**3)))


def striped8(idx):
    return np.concatenate([v.reshape(-1, 16).T for v in idx]).astype(np.uint16)


def unstriped8(offs):
    return np.stack([offs[16 * g:16 * g + 16].T.reshape(-1) for g in range(8)]).astype(np.int64)


def runs(v, idx8):
    k = np.arange(v.shape[0])
    return v[k[:, None], idx8[k % 512 // 64]]


def bf(x):
    return np.asarray(x, np.float32).astype(ml_dtypes.bfloat16)


def planes(Y):
    n, m = Y.shape
    b = f64(bf(Y)).reshape(n // 32, 32, m)
    amax = np.abs(b).max(1)
    byte = np.clip(np.where(amax > 0, np.frexp(amax)[1] - 1 + 127 - 7, 1), 1, 254)
    codes = (b * np.exp2(127.0 - byte)[:, None, :]).reshape(n, m).astype(np.float32).astype(ml_dtypes.float8_e4m3fn).view(np.uint8)
    words = codes.reshape(n // 512, 128, 4, m).transpose(0, 1, 3, 2)
    return np.ascontiguousarray(words), np.ascontiguousarray(byte.astype(np.uint8).reshape(n // 512, 16, m))


K, T, S, H, P = 1536, 2048, 1024, 512, 512

def setup_inputs():
    n = np.random.standard_normal
    s = mx_kscale(K)[:, None]
    u = mx_kscale(H)[:, None]
    d = {}
    d["tab_words"], d["tab_scales"] = pack_weight(n((K, T)) * s, "e4m3")
    d["w1_words"], d["w1_scales"] = pack_weight(n((K, H)) / K ** 0.5 / s, "e2m1")
    d["w2"] = (1.4 * n((K, H)) / K ** 0.5 / s).astype(np.float32)
    d["gain"] = (np.exp(0.3 * n(H)) * u[:, 0]).astype(np.float32)
    d["w3"] = (n((H, H)) / H ** 0.5 / u).astype(np.float32)
    d["rowgain"] = np.exp(0.8 * n(H)).astype(np.float32)
    d["offs"] = striped8(np.stack([np.random.permutation(T)[:S] for _ in range(8)]))
    d["pos1"] = striped(np.random.permutation(S)[:P])
    d["pos2"] = striped(np.random.permutation(S)[:P])
    return d

def reference(tab_words, tab_scales, w1_words, w1_scales, w2, gain, w3, rowgain, offs, pos1, pos2):
    v = runs(unpack_weight(tab_words, tab_scales, "e4m3"), unstriped8(offs))
    a = unpack_weight(w1_words, w1_scales, "e2m1").T @ v
    b = f64(gain)[:, None] * np.tanh(mxq(f64(w2), 0, "e4m3").T @ v)
    a1 = a[:, unstriped(pos1)]
    b2 = b[:, unstriped(pos2)]
    z = a1 * b2 + b2
    r = mxq(f64(w3), 0, "e4m3").T @ mxq(z, 0, "e4m3")
    y = f64(rowgain)[:, None] * (r + a1)
    words, scales = planes(y)
    return y, words, scales

@@ -1,0 +1,278 @@
+from contextlib import ExitStack
+
+import concourse.mybir as mybir
+
+K, T, S, H, PAIRS = 1536, 2048, 1024, 512, 512
+FLOPS = 2 * K * H * S * 2 + 2 * H * H * PAIRS
+
+F32 = mybir.dt.float32
+BF16 = mybir.dt.bfloat16
+I32 = mybir.dt.int32
+U32 = mybir.dt.uint32
+U16 = mybir.dt.uint16
+U8 = mybir.dt.uint8
+FP8X4 = mybir.dt.float8_e4m3fn_x4
+FP4X4 = mybir.dt.float4_e2m1fn_x4
+ACT = mybir.ActivationFunctionType
+ALU = mybir.AluOpType
+
+P = 128
+PACK = 4
+PASSES = K // (P * PACK)
+BANK = 512
+HALF = PAIRS // 2
+SLOT = 8192
+
+
+def copy_on(nc, eng, out, in_):
+    if eng == "scalar":
+        nc.scalar.copy(out=out, in_=in_)
+    elif eng == "vector":
+        nc.vector.tensor_copy(out=out, in_=in_)
+    else:
+        nc.gpsimd.tensor_scalar(out=out, in0=in_, scalar1=1.0, scalar2=0.0, op0=ALU.mult, op1=ALU.add)
+
+
+def tile_list_ring_steering_features_kernel(
+    tc, tab_words, tab_scales, w1_words, w1_scales, w2, gain, w3, rowgain, offs, pos1, pos2, out_0, out_1, out_2
+):
+    nc = tc.nc
+    with ExitStack() as ctx:
+        keep = ctx.enter_context(tc.tile_pool(name="keep", bufs=1))
+        stage = ctx.enter_context(tc.tile_pool(name="stage", bufs=1))
+        psum = ctx.enter_context(tc.psum_pool(name="psum", bufs=1))
+
+        offs_sb = keep.tile([P, S // 16], U16, name="offs_sb")
+        pos1_sb = keep.tile([P, PAIRS // 16], U16, name="pos1_sb")
+        pos2_sb = keep.tile([P, PAIRS // 16], U16, name="pos2_sb")
+        nc.sync.dma_start(offs_sb[:], offs)
+        w1w_raw = keep.tile([P, PASSES, H], U16, name="w1w_raw")
+        nc.sync.dma_start(w1w_raw[:].bitcast(I32), w1_words.rearrange("a p c -> p a c").bitcast(I32))
+        nc.sync.dma_start(pos1_sb[:], pos1)
+        nc.sync.dma_start(pos2_sb[:], pos2)
+
+        tscale = stage.tile([P, T], U8, name="tscale", offset=2 * SLOT)
+        nc.vector.memset(tscale[:].bitcast(I32), 0)
+        nc.scalar.dma_start(
+            tscale[:].bitcast(I32)[0:P:4, :], tab_scales[0:2].rearrange("a q c -> q a c").bitcast(I32)
+        )
+        nc.scalar.dma_start(tscale[:].bitcast(I32)[1:P:8, :], tab_scales[2].bitcast(I32))
+
+        def load_table(a):
+            words = stage.tile([P, T], U32, name=f"tab{a}", offset=a * SLOT)
+            nc.sync.dma_start(words[:].bitcast(I32), tab_words[a].rearrange("p n t -> p (n t)").bitcast(I32))
+            return words
+
+        tabs = [load_table(0), load_table(1)]
+
+        w1s_raw = keep.tile([P, PASSES, H], U8, name="w1s_raw")
+        nc.vector.memset(w1s_raw[:].bitcast(I32), 0)
+        for d in range(4):
+            nc.gpsimd.dma_start(
+                w1s_raw[:].bitcast(I32)[32 * d : 32 * d + 4, :, :],
+                w1_scales[:, 4 * d : 4 * d + 4, :].rearrange("a r c -> r a c").bitcast(I32),
+            )
+        gain_sb = keep.tile([P, PACK], F32, name="gain_sb")
+        rowgain_sb = keep.tile([P, PACK], F32, name="rowgain_sb")
+        nc.gpsimd.dma_start(gain_sb[:], gain.rearrange("(p t) -> p t", t=PACK))
+        nc.gpsimd.dma_start(rowgain_sb[:], rowgain.rearrange("(p t) -> p t", t=PACK))
+
+        plane01 = keep.tile([P, 2 * S], U8, name="vplane01", align_bytes=64)
+        plane2 = keep.tile([P, S], U8, name="vplane2", align_bytes=64)
+        nc.vector.memset(plane01[:].bitcast(I32), 0)
+        nc.vector.memset(plane2[:].bitcast(I32), 0)
+        planes = [plane01[:, 0:S], plane01[:, S : 2 * S], plane2[:]]
+
+        picked_scale = keep.tile([P, S], U8, name="picked_scale")
+        nc.vector.tensor_copy(picked_scale[:], tscale[:].indirect(offs_sb[:]))
+
+
+        for d in range(4):
+            nc.scalar.dma_start(
+                plane01[:].bitcast(I32)[32 * d : 32 * d + 4, :], picked_scale[:].bitcast(I32)[32 * d : 32 * d + 32 : 4, :]
+            )
+        for d in range(4):
+            nc.scalar.dma_start(
+                plane2[:].bitcast(I32)[32 * d : 32 * d + 4, :], picked_scale[:].bitcast(I32)[32 * d + 1 : 32 * d + 32 : 8, :]
+            )
+        tabs.append(load_table(2))
+
+        vwords = [keep.tile([P, S], U32, name=f"vwords{a}", align_bytes=64) for a in range(PASSES)]
+        nc.vector.tensor_copy(vwords[0][:], tabs[0][:].indirect(offs_sb[:]))
+
+        w1w = []
+        w1s = []
+        for a in range(PASSES):
+            words = keep.tile([P, 2 * H], U8, name=f"w1w{a}", align_bytes=64)
+            nc.scalar.copy(
+                out=words[:].bitcast(U16).rearrange("p (t m) -> p t m", t=PACK),
+                in_=w1w_raw[:, a, :].rearrange("p (m t) -> p t m", t=PACK),
+            )
+            w1w.append(words)
+        w1s_all = keep.tile([P, PASSES, H], U8, name="w1s_all", align_bytes=64)
+        nc.vector.tensor_copy(
+            out=w1s_all[:].rearrange("p a (t m) -> p a t m", t=PACK),
+            in_=w1s_raw[:].rearrange("p a (m t) -> p a t m", t=PACK),
+        )
+
+        nc.vector.tensor_copy(vwords[1][:], tabs[1][:].indirect(offs_sb[:]))
+        for h in range(2):
+            nc.vector.tensor_copy(
+                vwords[2][:, h * BANK : (h + 1) * BANK], tabs[2][:].indirect(offs_sb[:, 32 * h : 32 * h + 32])
+            )
+
+        def load_weight(name, rows, slot):
+            raw = stage.tile([P, PACK, H], F32, name=name, offset=slot * SLOT)
+            nc.sync.dma_start(raw[:], rows.rearrange("(p j) c -> p j c", j=PACK))
+            return raw
+
+        def deal_weight(name, raw, eng):
+            dealt = keep.tile([P, H * PACK], BF16, name=name, align_bytes=64)
+            copy_on(
+                nc,
+                eng,
+                dealt[:].rearrange("p (t m j) -> p m t j", t=PACK, j=PACK),
+                raw[:].rearrange("p j (m t) -> p m t j", t=PACK),
+            )
+            return dealt
+
+        def quantize(name, src, width):
+            codes = keep.tile([P, width], U32, name=name + "_codes", align_bytes=64)
+            scales = keep.tile([P, width], U8, name=name + "_scales", align_bytes=64)
+            nc.vector.quantize_mx(out=codes[:].bitcast(FP8X4), scales=scales[:], in_=src)
+            return codes, scales
+
+        w2_raw = [load_weight(f"w2raw{a}", w2[a * 512 : (a + 1) * 512, :], a) for a in range(PASSES)]
+
+        def first_stage_pass(acc, lhsT, lhsT_scale, a, h):
+            cols = slice(h * BANK, (h + 1) * BANK)
+            nc.tensor.matmul_mx(
+                out=acc[:],
+                lhsT=lhsT,
+                lhsT_scale=lhsT_scale,
+                rhs=vwords[a][:, cols].bitcast(FP8X4),
+                rhs_scale=planes[a][:, cols],
+                start=(a == 0),
+                stop=(a == PASSES - 1),
+            )
+
+        a_acc = [[psum.tile([P, BANK], F32, name=f"a{t}{h}", tag=f"bank{t}{h}") for h in range(2)] for t in range(PACK)]
+
+        def a_pass(t, a, h):
+            first_stage_pass(
+                a_acc[t][h], w1w[a][:, 2 * P * t : 2 * P * (t + 1)].bitcast(FP4X4), w1s_all[:, a, P * t : P * (t + 1)], a, h
+            )
+
+        for a in range(PASSES - 1):
+            for t in range(PACK):
+                for h in range(2):
+                    a_pass(t, a, h)
+        for t in range(PACK):
+            a_pass(t, PASSES - 1, 0)
+
+        w2_dealt0 = deal_weight("w2dealt0", w2_raw[0], "vector")
+        w3_raw = load_weight("w3raw", w3, 0)
+        w2_q = [quantize("w2q0", w2_dealt0[:], H)]
+
+        a1 = keep.tile([P, PACK, PAIRS], F32, name="a1")
+        u = keep.tile([P, PACK, PAIRS], F32, name="u")
+        a1g = keep.tile([P, PACK, PAIRS], F32, name="a1g")
+        for t in range(PACK):
+            a_pass(t, PASSES - 1, 1)
+            a_rows = keep.tile([P, S], F32, name=f"a_rows{t}")
+            for h in range(2):
+                nc.scalar.copy(out=a_rows[:, h * BANK : (h + 1) * BANK], in_=a_acc[t][h][:])
+            nc.vector.tensor_copy(a1[:, t, :], a_rows[:].indirect(pos1_sb[:]))
+
+        for a in range(1, PASSES):
+            dealt = deal_weight(f"w2dealt{a}", w2_raw[a], ["scalar", "vector"][a - 1])
+            w2_q.append(quantize(f"w2q{a}", dealt[:], H))
+
+        def scale_rows(out, t, factor, plus):
+            if plus:
+                nc.scalar.activation(out=out[:, t, :], in_=a1[:, t, :], func=ACT.Identity, scale=factor[:, t : t + 1], bias=factor[:, t : t + 1])
+            else:
+                nc.scalar.activation(out=out[:, t, :], in_=a1[:, t, :], func=ACT.Copy, scale=factor[:, t : t + 1])
+
+        for t in range(PACK):
+            scale_rows(u, t, gain_sb, True)
+
+        z = [keep.tile([P, PACK, HALF], F32, name=f"z{h}") for h in range(2)]
+        for t in range(PACK):
+            b_acc = [psum.tile([P, BANK], F32, name=f"b{t}{h}", tag=f"bank{t}{h}") for h in range(2)]
+            for a in range(PASSES):
+                codes, scales = w2_q[a]
+                for h in range(2):
+                    first_stage_pass(
+                        b_acc[h], codes[:, P * t : P * (t + 1)].bitcast(FP8X4), scales[:, P * t : P * (t + 1)], a, h
+                    )
+            b_rows = keep.tile([P, S], F32, name=f"b_rows{t}")
+            for h in range(2):
+                nc.scalar.activation(out=b_rows[:, h * BANK : (h + 1) * BANK], in_=b_acc[h][:], func=ACT.Tanh)
+            for h in range(2):
+                nc.vector.tensor_tensor(
+                    z[h][:, t, :],
+                    b_rows[:].indirect(pos2_sb[:, 16 * h : 16 * h + 16]),
+                    u[:, t, h * HALF : (h + 1) * HALF],
+                    ALU.mult,
+                )
+
+        w3_dealt = deal_weight("w3dealt", w3_raw, "scalar")
+        w3_codes, w3_scales = quantize("w3q", w3_dealt[:], H)
+        for t in range(PACK):
+            scale_rows(a1g, t, rowgain_sb, False)
+
+        def weave(name, src, eng):
+            woven = keep.tile([P, HALF * PACK], BF16, name=name, align_bytes=64)
+            copy_on(
+                nc,
+                eng,
+                woven[:].rearrange("p (c i t) -> p c t i", i=4, t=PACK),
+                src[:].rearrange("p t (c i) -> p c t i", i=4),
+            )
+            return woven
+
+        z_q = []
+        for h in range(2):
+            woven = weave(f"zw{h}", z[h], ["scalar", "scalar"][h])
+            z_q.append(quantize(f"zq{h}", woven[:], HALF))
+
+        y_codes = keep.tile([P, PAIRS], U32, name="y_codes", align_bytes=64)
+        y_scales = keep.tile([P, PAIRS], U8, name="y_scales", align_bytes=64)
+        out_rows = out_0.rearrange("(p t) m -> p t m", t=PACK)
+        out_words = out_1[0].rearrange("p m t -> p (m t)").bitcast(I32)
+        y = []
+        for h in range(2):
+            cols = slice(h * HALF, (h + 1) * HALF)
+            y_half = keep.tile([P, PACK, HALF], F32, name=f"y{h}")
+            for t in range(PACK):
+                r_acc = psum.tile([P, HALF], F32, name=f"r{t}{h}", tag=f"bank{t}{h}")
+                nc.tensor.matmul_mx(
+                    out=r_acc[:],
+                    lhsT=w3_codes[:, P * t : P * (t + 1)].bitcast(FP8X4),
+                    lhsT_scale=w3_scales[:, P * t : P * (t + 1)],
+                    rhs=z_q[h][0][:].bitcast(FP8X4),
+                    rhs_scale=z_q[h][1][:],
+                    start=True,
+                    stop=True,
+                )
+                nc.vector.scalar_tensor_tensor(
+                    out=y_half[:, t, :],
+                    in0=r_acc[:],
+                    scalar=rowgain_sb[:, t : t + 1],
+                    in1=a1g[:, t, cols],
+                    op0=ALU.mult,
+                    op1=ALU.add,
+                )
+            nc.sync.dma_start(out_rows[:, :, cols], y_half[:])
+            y.append(y_half)
+        for h in range(2):
+            cols = slice(h * HALF, (h + 1) * HALF)
+            woven = weave(f"yw{h}", y[h], ["scalar", "vector"][h])
+            nc.vector.quantize_mx(out=y_codes[:, cols].bitcast(FP8X4), scales=y_scales[:, cols], in_=woven[:])
+            nc.sync.dma_start(out_words[:, cols], y_codes[:, cols].bitcast(I32))
+        for d in range(4):
+            queue = nc.scalar if d % 2 else nc.sync
+            queue.dma_start(
+                out_2[0, 4 * d : 4 * d + 4, :].bitcast(I32), y_scales[:].bitcast(I32)[32 * d : 32 * d + 4, :]
+            )

@@ -22,6 +22,8 @@ PASSES = K // (P * PACK)
 BANK = 512
 HALF = PAIRS // 2
 SLOT = 8192
+TAB_AT = (2560, 10752, 18944)
+RAW_AT = (0, 10752, 18944)
 
 
 def copy_on(nc, eng, out, in_):
@@ -33,6 +35,20 @@ def copy_on(nc, eng, out, in_):
         nc.gpsimd.tensor_scalar(out=out, in0=in_, scalar1=1.0, scalar2=0.0, op0=ALU.mult, op1=ALU.add)
 
 
+def scale_on(nc, eng, out, in_, factor, plus):
+    if eng == "scalar":
+        if plus:
+            nc.scalar.activation(out=out, in_=in_, func=ACT.Identity, scale=factor, bias=factor)
+        else:
+            nc.scalar.activation(out=out, in_=in_, func=ACT.Copy, scale=factor)
+    else:
+        engine = nc.gpsimd if eng == "gpsimd" else nc.vector
+        if plus:
+            engine.tensor_scalar(out=out, in0=in_, scalar1=factor, scalar2=factor, op0=ALU.mult, op1=ALU.add)
+        else:
+            engine.tensor_scalar(out=out, in0=in_, scalar1=factor, scalar2=0.0, op0=ALU.mult, op1=ALU.add)
+
+
 def tile_list_ring_steering_features_kernel(
     tc, tab_words, tab_scales, w1_words, w1_scales, w2, gain, w3, rowgain, offs, pos1, pos2, out_0, out_1, out_2
 ):
@@ -40,66 +56,79 @@ def tile_list_ring_steering_features_kernel(
     with ExitStack() as ctx:
         keep = ctx.enter_context(tc.tile_pool(name="keep", bufs=1))
         stage = ctx.enter_context(tc.tile_pool(name="stage", bufs=1))
+        reuse = ctx.enter_context(tc.tile_pool(name="reuse", bufs=1))
         psum = ctx.enter_context(tc.psum_pool(name="psum", bufs=1))
 
         offs_sb = keep.tile([P, S // 16], U16, name="offs_sb")
         pos1_sb = keep.tile([P, PAIRS // 16], U16, name="pos1_sb")
         pos2_sb = keep.tile([P, PAIRS // 16], U16, name="pos2_sb")
         nc.sync.dma_start(offs_sb[:], offs)
-        w1w_raw = keep.tile([P, PASSES, H], U16, name="w1w_raw")
-        nc.sync.dma_start(w1w_raw[:].bitcast(I32), w1_words.rearrange("a p c -> p a c").bitcast(I32))
-        nc.sync.dma_start(pos1_sb[:], pos1)
-        nc.sync.dma_start(pos2_sb[:], pos2)
 
-        tscale = stage.tile([P, T], U8, name="tscale", offset=2 * SLOT)
-        nc.vector.memset(tscale[:].bitcast(I32), 0)
-        nc.scalar.dma_start(
-            tscale[:].bitcast(I32)[0:P:4, :], tab_scales[0:2].rearrange("a q c -> q a c").bitcast(I32)
+        tscale = stage.tile([P, T], U8, name="tscale", offset=TAB_AT[2])
+        tscale_words = tscale[:].bitcast(I32)
+        first_two = tab_scales[0:2].rearrange("a q c -> q a c").bitcast(I32)
+        nc.sync.dma_start(tscale_words[0:P:4, :], first_two)
+        nc.sync.dma_start(
+            tscale_words[1:P:2, :], tab_scales[2].bitcast(I32).unsqueeze(1).to_broadcast([16, 4, T // 4])
         )
-        nc.scalar.dma_start(tscale[:].bitcast(I32)[1:P:8, :], tab_scales[2].bitcast(I32))
+        nc.sync.dma_start(tscale_words[2:P:4, :], first_two)
 
         def load_table(a):
-            words = stage.tile([P, T], U32, name=f"tab{a}", offset=a * SLOT)
+            words = stage.tile([P, T], U32, name=f"tab{a}", offset=TAB_AT[a])
             nc.sync.dma_start(words[:].bitcast(I32), tab_words[a].rearrange("p n t -> p (n t)").bitcast(I32))
             return words
 
-        tabs = [load_table(0), load_table(1)]
-
-        w1s_raw = keep.tile([P, PASSES, H], U8, name="w1s_raw")
-        nc.vector.memset(w1s_raw[:].bitcast(I32), 0)
+        w1s_raw = reuse.tile([P, PASSES, H], U8, name="w1s_raw", offset=8192)
+        nc.gpsimd.memset(w1s_raw[:].bitcast(I32), 0)
         for d in range(4):
             nc.gpsimd.dma_start(
                 w1s_raw[:].bitcast(I32)[32 * d : 32 * d + 4, :, :],
                 w1_scales[:, 4 * d : 4 * d + 4, :].rearrange("a r c -> r a c").bitcast(I32),
             )
-        gain_sb = keep.tile([P, PACK], F32, name="gain_sb")
-        rowgain_sb = keep.tile([P, PACK], F32, name="rowgain_sb")
-        nc.gpsimd.dma_start(gain_sb[:], gain.rearrange("(p t) -> p t", t=PACK))
-        nc.gpsimd.dma_start(rowgain_sb[:], rowgain.rearrange("(p t) -> p t", t=PACK))
+        tabs = [load_table(0)]
+        nc.sync.dma_start(pos1_sb[:], pos1)
+        nc.sync.dma_start(pos2_sb[:], pos2)
+        tabs.append(load_table(1))
+        w1w_raw = keep.tile([P, PASSES, H], U16, name="w1w_raw")
+        nc.sync.dma_start(w1w_raw[:].bitcast(I32), w1_words.rearrange("a p c -> p a c").bitcast(I32))
+
 
         plane01 = keep.tile([P, 2 * S], U8, name="vplane01", align_bytes=64)
-        plane2 = keep.tile([P, S], U8, name="vplane2", align_bytes=64)
         nc.vector.memset(plane01[:].bitcast(I32), 0)
-        nc.vector.memset(plane2[:].bitcast(I32), 0)
-        planes = [plane01[:, 0:S], plane01[:, S : 2 * S], plane2[:]]
 
         picked_scale = keep.tile([P, S], U8, name="picked_scale")
         nc.vector.tensor_copy(picked_scale[:], tscale[:].indirect(offs_sb[:]))
-
-
+        picked_words = picked_scale[:].bitcast(I32)
         for d in range(4):
-            nc.scalar.dma_start(
-                plane01[:].bitcast(I32)[32 * d : 32 * d + 4, :], picked_scale[:].bitcast(I32)[32 * d : 32 * d + 32 : 4, :]
-            )
-        for d in range(4):
-            nc.scalar.dma_start(
-                plane2[:].bitcast(I32)[32 * d : 32 * d + 4, :], picked_scale[:].bitcast(I32)[32 * d + 1 : 32 * d + 32 : 8, :]
-            )
+            nc.sync.dma_start(plane01[:].bitcast(I32)[32 * d : 32 * d + 4, :], picked_words[32 * d : 32 * d + 32 : 4, :])
         tabs.append(load_table(2))
 
         vwords = [keep.tile([P, S], U32, name=f"vwords{a}", align_bytes=64) for a in range(PASSES)]
         nc.vector.tensor_copy(vwords[0][:], tabs[0][:].indirect(offs_sb[:]))
 
+        def load_weight(name, rows, slot):
+            raw = stage.tile([P, PACK, H], F32, name=name, offset=RAW_AT[slot])
+            nc.sync.dma_start(raw[:], rows.rearrange("(p j) c -> p j c", j=PACK))
+            return raw
+
+        w2_raw = [load_weight("w2raw0", w2[0:512, :], 0)]
+        plane2 = stage.tile([P, S], U8, name="vplane2", align_bytes=64, offset=8192)
+        nc.vector.memset(plane2[:].bitcast(I32), 0)
+        planes = [plane01[:, 0:S], plane01[:, S : 2 * S], plane2[:]]
+        for d in range(4):
+            nc.sync.dma_start(plane2[:].bitcast(I32)[32 * d : 32 * d + 4, :], picked_words[32 * d + 1 : 32 * d + 32 : 8, :])
+        w1s_dealt = []
+        for a in range(PASSES):
+            dealt_scales = keep.tile([P, H], U8, name=f"w1s{a}", align_bytes=64)
+            nc.gpsimd.tensor_copy(
+                out=dealt_scales[:].rearrange("p (t m) -> p t m", t=PACK),
+                in_=w1s_raw[:, a, :].rearrange("p (m t) -> p t m", t=PACK),
+            )
+            w1s_dealt.append(dealt_scales)
+        gain_sb = reuse.tile([P, PACK], F32, name="gain_sb", offset=8192)
+        rowgain_sb = reuse.tile([P, PACK], F32, name="rowgain_sb", offset=8192 + 64)
+        nc.gpsimd.dma_start(gain_sb[:], gain.rearrange("(p t) -> p t", t=PACK))
+        nc.gpsimd.dma_start(rowgain_sb[:], rowgain.rearrange("(p t) -> p t", t=PACK))
         w1w = []
         w1s = []
         for a in range(PASSES):
@@ -109,11 +138,8 @@ def tile_list_ring_steering_features_kernel(
                 in_=w1w_raw[:, a, :].rearrange("p (m t) -> p t m", t=PACK),
             )
             w1w.append(words)
-        w1s_all = keep.tile([P, PASSES, H], U8, name="w1s_all", align_bytes=64)
-        nc.vector.tensor_copy(
-            out=w1s_all[:].rearrange("p a (t m) -> p a t m", t=PACK),
-            in_=w1s_raw[:].rearrange("p a (m t) -> p a t m", t=PACK),
-        )
+            w1s.append(w1s_dealt[a])
+
 
         nc.vector.tensor_copy(vwords[1][:], tabs[1][:].indirect(offs_sb[:]))
         for h in range(2):
@@ -121,20 +147,13 @@ def tile_list_ring_steering_features_kernel(
                 vwords[2][:, h * BANK : (h + 1) * BANK], tabs[2][:].indirect(offs_sb[:, 32 * h : 32 * h + 32])
             )
 
-        def load_weight(name, rows, slot):
-            raw = stage.tile([P, PACK, H], F32, name=name, offset=slot * SLOT)
-            nc.sync.dma_start(raw[:], rows.rearrange("(p j) c -> p j c", j=PACK))
-            return raw
-
-        def deal_weight(name, raw, eng):
-            dealt = keep.tile([P, H * PACK], BF16, name=name, align_bytes=64)
+        def deal_weight(dealt, raw, eng, ms=slice(0, P), ts=slice(0, PACK)):
             copy_on(
                 nc,
                 eng,
-                dealt[:].rearrange("p (t m j) -> p m t j", t=PACK, j=PACK),
-                raw[:].rearrange("p j (m t) -> p m t j", t=PACK),
+                dealt[:].rearrange("p (t m j) -> p m t j", t=PACK, j=PACK)[:, ms, ts, :],
+                raw[:].rearrange("p j (m t) -> p m t j", t=PACK)[:, ms, ts, :],
             )
-            return dealt
 
         def quantize(name, src, width):
             codes = keep.tile([P, width], U32, name=name + "_codes", align_bytes=64)
@@ -142,9 +161,9 @@ def tile_list_ring_steering_features_kernel(
             nc.vector.quantize_mx(out=codes[:].bitcast(FP8X4), scales=scales[:], in_=src)
             return codes, scales
 
-        w2_raw = [load_weight(f"w2raw{a}", w2[a * 512 : (a + 1) * 512, :], a) for a in range(PASSES)]
+        w2_raw.extend(load_weight(f"w2raw{a}", w2[a * 512 : (a + 1) * 512, :], a) for a in range(1, PASSES))
 
-        def first_stage_pass(acc, lhsT, lhsT_scale, a, h):
+        def first_stage_pass(acc, lhsT, lhsT_scale, a, h, last):
             cols = slice(h * BANK, (h + 1) * BANK)
             nc.tensor.matmul_mx(
                 out=acc[:],
@@ -153,49 +172,71 @@ def tile_list_ring_steering_features_kernel(
                 rhs=vwords[a][:, cols].bitcast(FP8X4),
                 rhs_scale=planes[a][:, cols],
                 start=(a == 0),
-                stop=(a == PASSES - 1),
+                stop=last,
             )
 
         a_acc = [[psum.tile([P, BANK], F32, name=f"a{t}{h}", tag=f"bank{t}{h}") for h in range(2)] for t in range(PACK)]
 
-        def a_pass(t, a, h):
+        def a_pass(t, a, h, last):
             first_stage_pass(
-                a_acc[t][h], w1w[a][:, 2 * P * t : 2 * P * (t + 1)].bitcast(FP4X4), w1s_all[:, a, P * t : P * (t + 1)], a, h
+                a_acc[t][h], w1w[a][:, 2 * P * t : 2 * P * (t + 1)].bitcast(FP4X4), w1s[a][:, P * t : P * (t + 1)], a, h, last
             )
 
-        for a in range(PASSES - 1):
-            for t in range(PACK):
-                for h in range(2):
-                    a_pass(t, a, h)
         for t in range(PACK):
-            a_pass(t, PASSES - 1, 0)
-
-        w2_dealt0 = deal_weight("w2dealt0", w2_raw[0], "vector")
-        w3_raw = load_weight("w3raw", w3, 0)
-        w2_q = [quantize("w2q0", w2_dealt0[:], H)]
-
-        a1 = keep.tile([P, PACK, PAIRS], F32, name="a1")
-        u = keep.tile([P, PACK, PAIRS], F32, name="u")
-        a1g = keep.tile([P, PACK, PAIRS], F32, name="a1g")
-        for t in range(PACK):
-            a_pass(t, PASSES - 1, 1)
-            a_rows = keep.tile([P, S], F32, name=f"a_rows{t}")
             for h in range(2):
-                nc.scalar.copy(out=a_rows[:, h * BANK : (h + 1) * BANK], in_=a_acc[t][h][:])
-            nc.vector.tensor_copy(a1[:, t, :], a_rows[:].indirect(pos1_sb[:]))
+                a_pass(t, 0, h, False)
 
-        for a in range(1, PASSES):
-            dealt = deal_weight(f"w2dealt{a}", w2_raw[a], ["scalar", "vector"][a - 1])
-            w2_q.append(quantize(f"w2q{a}", dealt[:], H))
+        w2_dealt = [
+            reuse.tile([P, H * PACK], BF16, name="w2dealt0", align_bytes=64, offset=0),
+            keep.tile([P, H * PACK], BF16, name="w2dealt1", align_bytes=64),
+            reuse.tile([P, H * PACK], BF16, name="w2dealt2", align_bytes=64, offset=4096),
+        ]
+        deal_weight(w2_dealt[0], w2_raw[0], "vector")
+        w3_raw = load_weight("w3raw", w3, 0)
+        w2_q = [quantize("w2q0", w2_dealt[0][:], H)]
 
-        def scale_rows(out, t, factor, plus):
-            if plus:
-                nc.scalar.activation(out=out[:, t, :], in_=a1[:, t, :], func=ACT.Identity, scale=factor[:, t : t + 1], bias=factor[:, t : t + 1])
-            else:
-                nc.scalar.activation(out=out[:, t, :], in_=a1[:, t, :], func=ACT.Copy, scale=factor[:, t : t + 1])
-
+        a_rows = []
         for t in range(PACK):
-            scale_rows(u, t, gain_sb, True)
+            order = (1, 2) if t == 0 else (2, 1)
+            for a in order:
+                for h in range(2):
+                    a_pass(t, a, h, a == order[-1])
+            rows = keep.tile([P, S], F32, name=f"a_rows{t}")
+            for h in range(2):
+                nc.scalar.copy(out=rows[:, h * BANK : (h + 1) * BANK], in_=a_acc[t][h][:])
+            a_rows.append(rows)
+
+        a1 = [None] * PACK
+        u = [None] * PACK
+        ag = [None] * PACK
+
+        def pick_a(t, pool, offset):
+            a1[t] = pool.tile([P, PAIRS], F32, name=f"a1_{t}", offset=offset)
+            nc.vector.tensor_copy(a1[t][:], a_rows[t][:].indirect(pos1_sb[:]))
+
+        def make_u(t, pool, offset):
+            u[t] = pool.tile([P, PAIRS], F32, name=f"u{t}", offset=offset)
+            scale_on(nc, ["gpsimd","gpsimd","gpsimd","vector"][t], u[t][:], a1[t][:], gain_sb[:, t : t + 1], True)
+
+        def make_ag(t, pool, offset):
+            ag[t] = pool.tile([P, PAIRS], F32, name=f"ag{t}", offset=offset)
+            scale_on(nc, ["gpsimd","gpsimd","gpsimd","scalar"][t], ag[t][:], a1[t][:], rowgain_sb[:, t : t + 1], False)
+
+        deal_weight(w2_dealt[1], w2_raw[1], "gpsimd")
+        pick_a(0, reuse, 0)
+        pick_a(1, keep, None)
+        w2_q.append(quantize("w2q1", w2_dealt[1][:], H))
+        deal_weight(w2_dealt[2], w2_raw[2], "vector", ms=slice(0, P // 2))
+        deal_weight(w2_dealt[2], w2_raw[2], "scalar", ms=slice(P // 2, P))
+        w2_q.append(quantize("w2q2", w2_dealt[2][:], H))
+        for t in range(2):
+            make_u(t, stage, RAW_AT[1] + 4096 * t)
+            make_ag(t, stage, RAW_AT[1] + 4096 * t + 2048)
+        pick_a(2, reuse, 4096)
+        pick_a(3, reuse, 4096 + 2048)
+        make_u(2, keep, None)
+        make_ag(2, keep, None)
+        make_u(3, reuse, 12288)
 
         z = [keep.tile([P, PACK, HALF], F32, name=f"z{h}") for h in range(2)]
         for t in range(PACK):
@@ -204,7 +245,7 @@ def tile_list_ring_steering_features_kernel(
                 codes, scales = w2_q[a]
                 for h in range(2):
                     first_stage_pass(
-                        b_acc[h], codes[:, P * t : P * (t + 1)].bitcast(FP8X4), scales[:, P * t : P * (t + 1)], a, h
+                        b_acc[h], codes[:, P * t : P * (t + 1)].bitcast(FP8X4), scales[:, P * t : P * (t + 1)], a, h, a == PASSES - 1
                     )
             b_rows = keep.tile([P, S], F32, name=f"b_rows{t}")
             for h in range(2):
@@ -213,14 +254,15 @@ def tile_list_ring_steering_features_kernel(
                 nc.vector.tensor_tensor(
                     z[h][:, t, :],
                     b_rows[:].indirect(pos2_sb[:, 16 * h : 16 * h + 16]),
-                    u[:, t, h * HALF : (h + 1) * HALF],
+                    u[t][:, h * HALF : (h + 1) * HALF],
                     ALU.mult,
                 )
 
-        w3_dealt = deal_weight("w3dealt", w3_raw, "scalar")
+
+        w3_dealt = keep.tile([P, H * PACK], BF16, name="w3dealt", align_bytes=64)
+        for quarter in range(4):
+            deal_weight(w3_dealt, w3_raw, "scalar", ms=slice(32 * quarter, 32 * quarter + 32))
         w3_codes, w3_scales = quantize("w3q", w3_dealt[:], H)
-        for t in range(PACK):
-            scale_rows(a1g, t, rowgain_sb, False)
 
         def weave(name, src, eng):
             woven = keep.tile([P, HALF * PACK], BF16, name=name, align_bytes=64)
@@ -234,8 +276,9 @@ def tile_list_ring_steering_features_kernel(
 
         z_q = []
         for h in range(2):
-            woven = weave(f"zw{h}", z[h], ["scalar", "scalar"][h])
+            woven = weave(f"zw{h}", z[h], ["scalar","scalar"][h])
             z_q.append(quantize(f"zq{h}", woven[:], HALF))
+        make_ag(3, reuse, 13312)
 
         y_codes = keep.tile([P, PAIRS], U32, name="y_codes", align_bytes=64)
         y_scales = keep.tile([P, PAIRS], U8, name="y_scales", align_bytes=64)
@@ -260,7 +303,7 @@ def tile_list_ring_steering_features_kernel(
                     out=y_half[:, t, :],
                     in0=r_acc[:],
                     scalar=rowgain_sb[:, t : t + 1],
-                    in1=a1g[:, t, cols],
+                    in1=ag[t][:, cols],
                     op0=ALU.mult,
                     op1=ALU.add,
                 )
@@ -268,7 +311,7 @@ def tile_list_ring_steering_features_kernel(
             y.append(y_half)
         for h in range(2):
             cols = slice(h * HALF, (h + 1) * HALF)
-            woven = weave(f"yw{h}", y[h], ["scalar", "vector"][h])
+            woven = weave(f"yw{h}", y[h], ["scalar","vector"][h])
             nc.vector.quantize_mx(out=y_codes[:, cols].bitcast(FP8X4), scales=y_scales[:, cols], in_=woven[:])
             nc.sync.dma_start(out_words[:, cols], y_codes[:, cols].bitcast(I32))
         for d in range(4):

from contextlib import ExitStack

import concourse.mybir as mybir

K, T, S, H, PAIRS = 1536, 2048, 1024, 512, 512
FLOPS = 2 * K * H * S * 2 + 2 * H * H * PAIRS

F32 = mybir.dt.float32
BF16 = mybir.dt.bfloat16
I32 = mybir.dt.int32
U32 = mybir.dt.uint32
U16 = mybir.dt.uint16
U8 = mybir.dt.uint8
FP8X4 = mybir.dt.float8_e4m3fn_x4
FP4X4 = mybir.dt.float4_e2m1fn_x4
ACT = mybir.ActivationFunctionType
ALU = mybir.AluOpType

P = 128
PACK = 4
PASSES = K // (P * PACK)
BANK = 512
HALF = PAIRS // 2
SLOT = 8192
TAB_AT = (2560, 10752, 18944)
RAW_AT = (0, 10752, 18944)


def copy_on(nc, eng, out, in_):
    if eng == "scalar":
        nc.scalar.copy(out=out, in_=in_)
    elif eng == "vector":
        nc.vector.tensor_copy(out=out, in_=in_)
    else:
        nc.gpsimd.tensor_scalar(out=out, in0=in_, scalar1=1.0, scalar2=0.0, op0=ALU.mult, op1=ALU.add)


def scale_on(nc, eng, out, in_, factor, plus):
    if eng == "scalar":
        if plus:
            nc.scalar.activation(out=out, in_=in_, func=ACT.Identity, scale=factor, bias=factor)
        else:
            nc.scalar.activation(out=out, in_=in_, func=ACT.Copy, scale=factor)
    else:
        engine = nc.gpsimd if eng == "gpsimd" else nc.vector
        if plus:
            engine.tensor_scalar(out=out, in0=in_, scalar1=factor, scalar2=factor, op0=ALU.mult, op1=ALU.add)
        else:
            engine.tensor_scalar(out=out, in0=in_, scalar1=factor, scalar2=0.0, op0=ALU.mult, op1=ALU.add)


def tile_list_ring_steering_features_kernel(
    tc, tab_words, tab_scales, w1_words, w1_scales, w2, gain, w3, rowgain, offs, pos1, pos2, out_0, out_1, out_2
):
    nc = tc.nc
    with ExitStack() as ctx:
        keep = ctx.enter_context(tc.tile_pool(name="keep", bufs=1))
        stage = ctx.enter_context(tc.tile_pool(name="stage", bufs=1))
        reuse = ctx.enter_context(tc.tile_pool(name="reuse", bufs=1))
        psum = ctx.enter_context(tc.psum_pool(name="psum", bufs=1))

        offs_sb = keep.tile([P, S // 16], U16, name="offs_sb")
        pos1_sb = keep.tile([P, PAIRS // 16], U16, name="pos1_sb")
        pos2_sb = keep.tile([P, PAIRS // 16], U16, name="pos2_sb")
        nc.sync.dma_start(offs_sb[:], offs)

        tscale = stage.tile([P, T], U8, name="tscale", offset=TAB_AT[2])
        tscale_words = tscale[:].bitcast(I32)
        first_two = tab_scales[0:2].rearrange("a q c -> q a c").bitcast(I32)
        nc.sync.dma_start(tscale_words[0:P:4, :], first_two)
        nc.sync.dma_start(
            tscale_words[1:P:2, :], tab_scales[2].bitcast(I32).unsqueeze(1).to_broadcast([16, 4, T // 4])
        )
        nc.sync.dma_start(tscale_words[2:P:4, :], first_two)

        def load_table(a):
            words = stage.tile([P, T], U32, name=f"tab{a}", offset=TAB_AT[a])
            nc.sync.dma_start(words[:].bitcast(I32), tab_words[a].rearrange("p n t -> p (n t)").bitcast(I32))
            return words

        w1s_raw = reuse.tile([P, PASSES, H], U8, name="w1s_raw", offset=8192)
        nc.gpsimd.memset(w1s_raw[:].bitcast(I32), 0)
        for d in range(4):
            nc.gpsimd.dma_start(
                w1s_raw[:].bitcast(I32)[32 * d : 32 * d + 4, :, :],
                w1_scales[:, 4 * d : 4 * d + 4, :].rearrange("a r c -> r a c").bitcast(I32),
            )
        tabs = [load_table(0)]
        nc.sync.dma_start(pos1_sb[:], pos1)
        nc.sync.dma_start(pos2_sb[:], pos2)
        tabs.append(load_table(1))
        w1w_raw = keep.tile([P, PASSES, H], U16, name="w1w_raw")
        nc.sync.dma_start(w1w_raw[:].bitcast(I32), w1_words.rearrange("a p c -> p a c").bitcast(I32))


        plane01 = keep.tile([P, 2 * S], U8, name="vplane01", align_bytes=64)
        nc.vector.memset(plane01[:].bitcast(I32), 0)

        picked_scale = keep.tile([P, S], U8, name="picked_scale")
        nc.vector.tensor_copy(picked_scale[:], tscale[:].indirect(offs_sb[:]))
        picked_words = picked_scale[:].bitcast(I32)
        for d in range(4):
            nc.sync.dma_start(plane01[:].bitcast(I32)[32 * d : 32 * d + 4, :], picked_words[32 * d : 32 * d + 32 : 4, :])
        tabs.append(load_table(2))

        vwords = [keep.tile([P, S], U32, name=f"vwords{a}", align_bytes=64) for a in range(PASSES)]
        nc.vector.tensor_copy(vwords[0][:], tabs[0][:].indirect(offs_sb[:]))

        def load_weight(name, rows, slot):
            raw = stage.tile([P, PACK, H], F32, name=name, offset=RAW_AT[slot])
            nc.sync.dma_start(raw[:], rows.rearrange("(p j) c -> p j c", j=PACK))
            return raw

        w2_raw = [load_weight("w2raw0", w2[0:512, :], 0)]
        plane2 = stage.tile([P, S], U8, name="vplane2", align_bytes=64, offset=8192)
        nc.vector.memset(plane2[:].bitcast(I32), 0)
        planes = [plane01[:, 0:S], plane01[:, S : 2 * S], plane2[:]]
        for d in range(4):
            nc.sync.dma_start(plane2[:].bitcast(I32)[32 * d : 32 * d + 4, :], picked_words[32 * d + 1 : 32 * d + 32 : 8, :])
        w1s_dealt = []
        for a in range(PASSES):
            dealt_scales = keep.tile([P, H], U8, name=f"w1s{a}", align_bytes=64)
            nc.gpsimd.tensor_copy(
                out=dealt_scales[:].rearrange("p (t m) -> p t m", t=PACK),
                in_=w1s_raw[:, a, :].rearrange("p (m t) -> p t m", t=PACK),
            )
            w1s_dealt.append(dealt_scales)
        gain_sb = reuse.tile([P, PACK], F32, name="gain_sb", offset=8192)
        rowgain_sb = reuse.tile([P, PACK], F32, name="rowgain_sb", offset=8192 + 64)
        nc.gpsimd.dma_start(gain_sb[:], gain.rearrange("(p t) -> p t", t=PACK))
        nc.gpsimd.dma_start(rowgain_sb[:], rowgain.rearrange("(p t) -> p t", t=PACK))
        w1w = []
        w1s = []
        for a in range(PASSES):
            words = keep.tile([P, 2 * H], U8, name=f"w1w{a}", align_bytes=64)
            nc.scalar.copy(
                out=words[:].bitcast(U16).rearrange("p (t m) -> p t m", t=PACK),
                in_=w1w_raw[:, a, :].rearrange("p (m t) -> p t m", t=PACK),
            )
            w1w.append(words)
            w1s.append(w1s_dealt[a])


        nc.vector.tensor_copy(vwords[1][:], tabs[1][:].indirect(offs_sb[:]))
        for h in range(2):
            nc.vector.tensor_copy(
                vwords[2][:, h * BANK : (h + 1) * BANK], tabs[2][:].indirect(offs_sb[:, 32 * h : 32 * h + 32])
            )

        def deal_weight(dealt, raw, eng, ms=slice(0, P), ts=slice(0, PACK)):
            copy_on(
                nc,
                eng,
                dealt[:].rearrange("p (t m j) -> p m t j", t=PACK, j=PACK)[:, ms, ts, :],
                raw[:].rearrange("p j (m t) -> p m t j", t=PACK)[:, ms, ts, :],
            )

        def quantize(name, src, width):
            codes = keep.tile([P, width], U32, name=name + "_codes", align_bytes=64)
            scales = keep.tile([P, width], U8, name=name + "_scales", align_bytes=64)
            nc.vector.quantize_mx(out=codes[:].bitcast(FP8X4), scales=scales[:], in_=src)
            return codes, scales

        w2_raw.extend(load_weight(f"w2raw{a}", w2[a * 512 : (a + 1) * 512, :], a) for a in range(1, PASSES))

        def first_stage_pass(acc, lhsT, lhsT_scale, a, h, last):
            cols = slice(h * BANK, (h + 1) * BANK)
            nc.tensor.matmul_mx(
                out=acc[:],
                lhsT=lhsT,
                lhsT_scale=lhsT_scale,
                rhs=vwords[a][:, cols].bitcast(FP8X4),
                rhs_scale=planes[a][:, cols],
                start=(a == 0),
                stop=last,
            )

        a_acc = [[psum.tile([P, BANK], F32, name=f"a{t}{h}", tag=f"bank{t}{h}") for h in range(2)] for t in range(PACK)]

        def a_pass(t, a, h, last):
            first_stage_pass(
                a_acc[t][h], w1w[a][:, 2 * P * t : 2 * P * (t + 1)].bitcast(FP4X4), w1s[a][:, P * t : P * (t + 1)], a, h, last
            )

        for t in range(PACK):
            for h in range(2):
                a_pass(t, 0, h, False)

        w2_dealt = [
            reuse.tile([P, H * PACK], BF16, name="w2dealt0", align_bytes=64, offset=0),
            keep.tile([P, H * PACK], BF16, name="w2dealt1", align_bytes=64),
            reuse.tile([P, H * PACK], BF16, name="w2dealt2", align_bytes=64, offset=4096),
        ]
        deal_weight(w2_dealt[0], w2_raw[0], "vector")
        w3_raw = load_weight("w3raw", w3, 0)
        w2_q = [quantize("w2q0", w2_dealt[0][:], H)]

        a_rows = []
        for t in range(PACK):
            order = (1, 2) if t == 0 else (2, 1)
            for a in order:
                for h in range(2):
                    a_pass(t, a, h, a == order[-1])
            rows = keep.tile([P, S], F32, name=f"a_rows{t}")
            for h in range(2):
                nc.scalar.copy(out=rows[:, h * BANK : (h + 1) * BANK], in_=a_acc[t][h][:])
            a_rows.append(rows)

        a1 = [None] * PACK
        u = [None] * PACK
        ag = [None] * PACK

        def pick_a(t, pool, offset):
            a1[t] = pool.tile([P, PAIRS], F32, name=f"a1_{t}", offset=offset)
            nc.vector.tensor_copy(a1[t][:], a_rows[t][:].indirect(pos1_sb[:]))

        def make_u(t, pool, offset):
            u[t] = pool.tile([P, PAIRS], F32, name=f"u{t}", offset=offset)
            scale_on(nc, ["gpsimd","gpsimd","gpsimd","vector"][t], u[t][:], a1[t][:], gain_sb[:, t : t + 1], True)

        def make_ag(t, pool, offset):
            ag[t] = pool.tile([P, PAIRS], F32, name=f"ag{t}", offset=offset)
            scale_on(nc, ["gpsimd","gpsimd","gpsimd","scalar"][t], ag[t][:], a1[t][:], rowgain_sb[:, t : t + 1], False)

        deal_weight(w2_dealt[1], w2_raw[1], "gpsimd")
        pick_a(0, reuse, 0)
        pick_a(1, keep, None)
        w2_q.append(quantize("w2q1", w2_dealt[1][:], H))
        deal_weight(w2_dealt[2], w2_raw[2], "vector", ms=slice(0, P // 2))
        deal_weight(w2_dealt[2], w2_raw[2], "scalar", ms=slice(P // 2, P))
        w2_q.append(quantize("w2q2", w2_dealt[2][:], H))
        for t in range(2):
            make_u(t, stage, RAW_AT[1] + 4096 * t)
            make_ag(t, stage, RAW_AT[1] + 4096 * t + 2048)
        pick_a(2, reuse, 4096)
        pick_a(3, reuse, 4096 + 2048)
        make_u(2, keep, None)
        make_ag(2, keep, None)
        make_u(3, reuse, 12288)

        z = [keep.tile([P, PACK, HALF], F32, name=f"z{h}") for h in range(2)]
        for t in range(PACK):
            b_acc = [psum.tile([P, BANK], F32, name=f"b{t}{h}", tag=f"bank{t}{h}") for h in range(2)]
            for a in range(PASSES):
                codes, scales = w2_q[a]
                for h in range(2):
                    first_stage_pass(
                        b_acc[h], codes[:, P * t : P * (t + 1)].bitcast(FP8X4), scales[:, P * t : P * (t + 1)], a, h, a == PASSES - 1
                    )
            b_rows = keep.tile([P, S], F32, name=f"b_rows{t}")
            for h in range(2):
                nc.scalar.activation(out=b_rows[:, h * BANK : (h + 1) * BANK], in_=b_acc[h][:], func=ACT.Tanh)
            for h in range(2):
                nc.vector.tensor_tensor(
                    z[h][:, t, :],
                    b_rows[:].indirect(pos2_sb[:, 16 * h : 16 * h + 16]),
                    u[t][:, h * HALF : (h + 1) * HALF],
                    ALU.mult,
                )


        w3_dealt = keep.tile([P, H * PACK], BF16, name="w3dealt", align_bytes=64)
        for quarter in range(4):
            deal_weight(w3_dealt, w3_raw, "scalar", ms=slice(32 * quarter, 32 * quarter + 32))
        w3_codes, w3_scales = quantize("w3q", w3_dealt[:], H)

        def weave(name, src, eng):
            woven = keep.tile([P, HALF * PACK], BF16, name=name, align_bytes=64)
            copy_on(
                nc,
                eng,
                woven[:].rearrange("p (c i t) -> p c t i", i=4, t=PACK),
                src[:].rearrange("p t (c i) -> p c t i", i=4),
            )
            return woven

        z_q = []
        for h in range(2):
            woven = weave(f"zw{h}", z[h], ["scalar","scalar"][h])
            z_q.append(quantize(f"zq{h}", woven[:], HALF))
        make_ag(3, reuse, 13312)

        y_codes = keep.tile([P, PAIRS], U32, name="y_codes", align_bytes=64)
        y_scales = keep.tile([P, PAIRS], U8, name="y_scales", align_bytes=64)
        out_rows = out_0.rearrange("(p t) m -> p t m", t=PACK)
        out_words = out_1[0].rearrange("p m t -> p (m t)").bitcast(I32)
        y = []
        for h in range(2):
            cols = slice(h * HALF, (h + 1) * HALF)
            y_half = keep.tile([P, PACK, HALF], F32, name=f"y{h}")
            for t in range(PACK):
                r_acc = psum.tile([P, HALF], F32, name=f"r{t}{h}", tag=f"bank{t}{h}")
                nc.tensor.matmul_mx(
                    out=r_acc[:],
                    lhsT=w3_codes[:, P * t : P * (t + 1)].bitcast(FP8X4),
                    lhsT_scale=w3_scales[:, P * t : P * (t + 1)],
                    rhs=z_q[h][0][:].bitcast(FP8X4),
                    rhs_scale=z_q[h][1][:],
                    start=True,
                    stop=True,
                )
                nc.vector.scalar_tensor_tensor(
                    out=y_half[:, t, :],
                    in0=r_acc[:],
                    scalar=rowgain_sb[:, t : t + 1],
                    in1=ag[t][:, cols],
                    op0=ALU.mult,
                    op1=ALU.add,
                )
            nc.sync.dma_start(out_rows[:, :, cols], y_half[:])
            y.append(y_half)
        for h in range(2):
            cols = slice(h * HALF, (h + 1) * HALF)
            woven = weave(f"yw{h}", y[h], ["scalar","vector"][h])
            nc.vector.quantize_mx(out=y_codes[:, cols].bitcast(FP8X4), scales=y_scales[:, cols], in_=woven[:])
            nc.sync.dma_start(out_words[:, cols], y_codes[:, cols].bitcast(I32))
        for d in range(4):
            queue = nc.scalar if d % 2 else nc.sync
            queue.dma_start(
                out_2[0, 4 * d : 4 * d + 4, :].bitcast(I32), y_scales[:].bitcast(I32)[32 * d : 32 * d + 4, :]
            )
